import numpy as np
import ml_dtypes


def mxq(x, axis, fmt="e4m3"):
    dtype, down = {"e4m3": (ml_dtypes.float8_e4m3fn, 7), "e5m2": (ml_dtypes.float8_e5m2, 14)}[fmt]
    v = np.moveaxis(np.asarray(x, np.float32).astype(ml_dtypes.bfloat16).astype(np.float64), axis, -1)
    blocks = v.reshape(v.shape[:-1] + (-1, 32))
    amax = np.abs(blocks).max(-1, keepdims=True)
    byte = np.maximum(np.where(amax > 0, np.frexp(amax)[1] - 1 + 127, 0) - down, 1)
    scale = np.exp2(byte - 127.0)
    codes = (blocks / scale).astype(np.float32).astype(dtype).astype(np.float64)
    return np.moveaxis((codes * scale).reshape(v.shape), -1, axis)


WIDE = False


def mx_kscale(k):
    if not WIDE:
        return np.ones(k)
    levels = np.array([10, -10, 5, -5, 0])
    if k % 512:
        return np.exp2(np.random.permutation(np.resize(levels, k // 32))).repeat(32)
    a = np.empty((k // 512, 16))
    for p in range(k // 512):
        a[p, :8] = np.random.permutation(np.resize(levels, 8))
        for g in range(8):
            far = levels[np.abs(levels - a[p, g]) >= 10]
            a[p, g + 8] = far[np.random.randint(len(far))]
    return np.exp2(a.ravel()).repeat(32)


def f64(x):
    return np.asarray(x).astype(np.float64)


E2M1 = np.array([0.0, 0.5, 1.0, 1.5, 2.0, 3.0, 4.0, 6.0, -0.0, -0.5, -1.0, -1.5, -2.0, -3.0, -4.0, -6.0])


def pack_weight(w, fmt):
    k, n = w.shape
    w = f64(np.asarray(w, np.float32).astype(ml_dtypes.bfloat16)).reshape(k // 32, 32, n)
    amax = np.abs(w).max(1)
    if fmt == "e4m3":
        byte = np.frexp(amax)[1] - 1 + 127 - 7
    else:
        mant, ex = np.frexp(amax / 6.0)
        byte = np.where(mant > 0.5, ex, ex - 1) + 127
    byte = np.clip(np.where(amax > 0, byte, 1), 1, 254)
    scaled = (w * np.exp2(127.0 - byte)[:, None, :]).reshape(k, n).astype(np.float32)
    by_word = np.ascontiguousarray(scaled.reshape(k // 512, 128, 4, n).transpose(0, 1, 3, 2))
    if fmt == "e4m3":
        words = by_word.astype(ml_dtypes.float8_e4m3fn).view(np.uint8)
    else:
        c = by_word.astype(ml_dtypes.float4_e2m1fn).view(np.uint8) & 0xF
        words = (c[..., 0::2] | (c[..., 1::2] << 4)).reshape(k // 512, 128, 2 * n)
    return np.ascontiguousarray(words), np.ascontiguousarray(byte.astype(np.uint8).reshape(k // 512, 16, n))


def unpack_weight(words, scales, fmt):
    g, _, n = scales.shape
    words = np.ascontiguousarray(words).reshape(g, 128, n, -1)
    if fmt == "e4m3":
        vals = words.view(ml_dtypes.float8_e4m3fn).astype(np.float64)
    else:
        nib = np.empty((g, 128, n, 4), np.uint8)
        nib[..., 0::2] = words & 0xF
        nib[..., 1::2] = words >> 4
        vals = E2M1[nib]
    vals = vals * np.repeat(np.exp2(scales.astype(np.float64) - 127.0), 8, axis=1)[..., None]
    return vals.transpose(0, 1, 3, 2).reshape(g * 512, n)


def planes(y):
    n, m = y.shape
    v = y.astype(np.float32).astype(ml_dtypes.bfloat16).astype(np.float64).reshape(n // 32, 32, m)
    top = np.abs(v).max(1)
    byte = np.clip(np.where(top > 0, np.frexp(top)[1] - 1 + 127 - 7, 1), 1, 254)
    codes = (v * np.exp2(127.0 - byte)[:, None, :]).reshape(n, m).astype(np.float32).astype(ml_dtypes.float8_e4m3fn).view(np.uint8)
    words = codes.reshape(n // 512, 128, 4, m).transpose(0, 1, 3, 2)
    return np.ascontiguousarray(words), np.ascontiguousarray(byte.astype(np.uint8).reshape(n // 512, 16, m))


K, M, T = 512, 1536, 1024


def setup_inputs():
    n = np.random.standard_normal
    s = mx_kscale(K)[:, None]
    p_w4 = pack_weight(n((K, M)) / np.sqrt(K) / s, "e2m1")
    p_w8 = pack_weight(n((K, M)) / np.sqrt(K) / s, "e4m3")
    return {
        "x": (n((K, T)) * s).astype(np.float32),
        "w4_words": p_w4[0],
        "w4_scales": p_w4[1],
        "w8_words": p_w8[0],
        "w8_scales": p_w8[1],
    }


def reference(x, w4_words, w4_scales, w8_words, w8_scales):
    xa_, xb_ = mxq(np.maximum(f64(x), 0.0), 0, "e4m3"), mxq(np.maximum(-f64(x), 0.0), 0, "e4m3")
    w4_ = unpack_weight(w4_words, w4_scales, "e2m1")
    w8_ = unpack_weight(w8_words, w8_scales, "e4m3")
    y = w4_.T @ xa_ + w8_.T @ xb_
    out_0 = np.maximum(y, 0.0) ** 2
    return (out_0,) + planes(out_0)

@@ -1,0 +1,289 @@
+from contextlib import ExitStack
+
+import concourse.mybir as mybir
+
+K, M, T = 512, 1536, 1024
+FLOPS = 2 * 2 * K * M * T
+
+F32 = mybir.dt.float32
+BF16 = mybir.dt.bfloat16
+I32 = mybir.dt.int32
+U8 = mybir.dt.uint8
+FP8X4 = mybir.dt.float8_e4m3fn_x4
+FP4X4 = mybir.dt.float4_e2m1fn_x4
+ALU = mybir.AluOpType
+ACT = mybir.ActivationFunctionType
+
+P = 128
+PACK = 4
+GROUP = P * PACK
+GROUPS = M // GROUP
+CHUNK = 512
+CHUNKS = T // CHUNK
+HALF = CHUNK // 2
+RUN = 4
+UNITS = GROUPS * CHUNKS
+BANKS = 8
+W8_ROW = 4
+
+
+def tile_mix_feat_fm_crelupl_relu2_kernel(
+    tc, x, w4_words, w4_scales, w8_words, w8_scales, out_0, out_1, out_2
+):
+    nc = tc.nc
+    x_rows = x.rearrange("(p j) t -> p j t", j=PACK)
+    w4_bytes = w4_words[0]
+    w8_bytes = w8_words[0].rearrange("p n i -> p (n i)")
+
+    with ExitStack() as ctx:
+        keep = ctx.enter_context(tc.tile_pool(name="keep", bufs=1))
+        psum = ctx.enter_context(tc.psum_pool(name="psum", bufs=BANKS))
+        ctx.enter_context(tc.manual_schedule())
+
+        def sbuf(name, shape, dtype):
+            return keep.tile(shape, dtype, name=name, align_bytes=64)
+
+        x_raw = [sbuf("x_raw%d" % h, [P, PACK, HALF], F32) for h in range(2 * CHUNKS)]
+        feat = [[sbuf("feat%d_%d" % (s, c), [P, CHUNK, PACK], BF16) for c in range(CHUNKS)] for s in range(2)]
+        feat_codes = [[sbuf("fcode%d_%d" % (s, c), [P, CHUNK], I32) for c in range(CHUNKS)] for s in range(2)]
+        feat_scales = [[sbuf("fscale%d_%d" % (s, c), [P, CHUNK], U8) for c in range(CHUNKS)] for s in range(2)]
+        w4_first = sbuf("w4_first", [P, 2 * GROUP], U8)
+        w4_rest = sbuf("w4_rest", [P, 2 * (M - GROUP)], U8)
+        w8_first = sbuf("w8_first", [P, GROUP], I32)
+        w8_rest = sbuf("w8_rest", [P, M - GROUP], I32)
+        scale_raw = sbuf("scale_raw", [P, M], U8)
+        w4_dealt = [sbuf("w4_dealt%d" % a, [P, 2 * GROUP], U8) for a in range(GROUPS)]
+        w8_dealt = [sbuf("w8_dealt%d" % a, [P, GROUP], I32) for a in range(GROUPS)]
+        scale_dealt = [sbuf("scale_dealt%d" % a, [P, GROUP], U8) for a in range(GROUPS)]
+        relu = [sbuf("relu%d" % u, [P, PACK, CHUNK], F32) for u in range(UNITS)]
+        res = [sbuf("res%d" % u, [P, PACK, CHUNK], F32) for u in range(UNITS)]
+        res_bf = [sbuf("res_bf%d" % u, [P, CHUNK, PACK], BF16) for u in range(UNITS)]
+        res_codes = [sbuf("res_codes%d" % u, [P, CHUNK], I32) for u in range(UNITS)]
+        res_scales = [sbuf("res_scales%d" % c, [P, GROUPS, CHUNK], U8) for c in range(CHUNKS)]
+        acc = {}
+
+        def load_x(h):
+            nc.sync.dma_start(out=x_raw[h][:], in_=x_rows[:, :, h * HALF : (h + 1) * HALF])
+
+        def load_scales(queue, src, row):
+            for q in range(4):
+                queue.dma_start(
+                    out=scale_raw[32 * q + row : 32 * q + row + 4, :].bitcast(I32),
+                    in_=src[0, 4 * q : 4 * q + 4, :].bitcast(I32),
+                )
+
+        def interleaved(dst, src):
+            return (
+                dst.rearrange("p (c e) j -> p c j e", e=RUN),
+                src.rearrange("p j (c e) -> p c j e", e=RUN),
+            )
+
+        def feature_views(s, h):
+            c, part = divmod(h, 2)
+            return interleaved(feat[s][c][:, part * HALF : (part + 1) * HALF, :], x_raw[h][:])
+
+        def feature_on_vector(s, h):
+            dst, src = feature_views(s, h)
+            nc.vector.tensor_scalar(
+                out=dst, in0=src, scalar1=(1.0, -1.0)[s], scalar2=0.0, op0=ALU.mult, op1=ALU.max
+            )
+
+        def feature_on_scalar(s, h):
+            dst, src = feature_views(s, h)
+            nc.scalar.activation(out=dst, in_=src, func=ACT.Relu, scale=(1.0, -1.0)[s])
+
+        def quantize_feature(s, c):
+            nc.vector.quantize_mx(
+                out=feat_codes[s][c][:].bitcast(FP8X4),
+                scales=feat_scales[s][c][:],
+                in_=feat[s][c][:].rearrange("p t j -> p (t j)"),
+            )
+
+        def deal_w4(a):
+            src = w4_first[:] if a == 0 else w4_rest[:, 2 * GROUP * (a - 1) : 2 * GROUP * a]
+            nc.vector.tensor_copy(
+                out=w4_dealt[a][:].rearrange("p (r m b) -> p r m b", r=PACK, b=2),
+                in_=src.rearrange("p (m r b) -> p r m b", r=PACK, b=2),
+            )
+
+        def deal_w8(a):
+            src = w8_first[:] if a == 0 else w8_rest[:, GROUP * (a - 1) : GROUP * a]
+            nc.vector.tensor_copy(
+                out=w8_dealt[a][:].rearrange("p (r c e) -> p c r e", r=PACK, e=RUN),
+                in_=src.rearrange("p (c e r) -> p c r e", r=PACK, e=RUN),
+            )
+
+        def deal_scales(a):
+            nc.vector.tensor_copy(
+                out=scale_dealt[a][:].rearrange("p (r m) -> p r m", r=PACK),
+                in_=scale_raw[:, GROUP * a : GROUP * (a + 1)].rearrange("p (m r) -> p r m", r=PACK),
+            )
+
+        def pass_w4(b):
+            c, a = divmod(b // PACK, GROUPS)
+            r = b % PACK
+            acc[b] = psum.tile([P, CHUNK], F32, name="acc")
+            nc.tensor.matmul_mx(
+                out=acc[b][:],
+                lhsT=w4_dealt[a][:, 2 * P * r : 2 * P * (r + 1)].bitcast(FP4X4),
+                lhsT_scale=scale_dealt[a][:, P * r : P * (r + 1)],
+                rhs=feat_codes[0][c][:].bitcast(FP8X4),
+                rhs_scale=feat_scales[0][c][:],
+                start=True,
+                stop=False,
+            )
+
+        def pass_w8(b):
+            c, a = divmod(b // PACK, GROUPS)
+            r = b % PACK
+            nc.tensor.matmul_mx(
+                out=acc[b][:],
+                lhsT=w8_dealt[a][:, P * r : P * (r + 1)].bitcast(FP8X4),
+                lhsT_scale=scale_dealt[a][W8_ROW:P, P * r : P * (r + 1)],
+                rhs=feat_codes[1][c][:].bitcast(FP8X4),
+                rhs_scale=feat_scales[1][c][:],
+                start=False,
+                stop=True,
+            )
+
+        def both_passes(b):
+            if b < UNITS * PACK:
+                pass_w4(b)
+                pass_w8(b)
+
+        def drain(b, on_vector):
+            u, r = divmod(b, PACK)
+            if on_vector:
+                nc.vector.tensor_scalar_max(out=relu[u][:, r, :], in0=acc[b][:], scalar1=0.0)
+            else:
+                nc.scalar.activation(out=relu[u][:, r, :], in_=acc[b][:], func=ACT.Relu)
+            both_passes(b + BANKS)
+
+        def square(u, rows, cols, on_vector):
+            src = relu[u][:, rows, cols]
+            if on_vector:
+                nc.vector.tensor_tensor(out=res[u][:, rows, cols], in0=src, in1=src, op=ALU.mult)
+            else:
+                nc.scalar.activation(out=res[u][:, rows, cols], in_=src, func=ACT.Square)
+
+        def store_res(u, rows, cols):
+            c, a = divmod(u, GROUPS)
+            dst = out_0[GROUP * a : GROUP * (a + 1), CHUNK * c : CHUNK * (c + 1)]
+            nc.sync.dma_start(
+                out=dst.rearrange("(p r) t -> p r t", r=PACK)[:, rows, cols], in_=res[u][:, rows, cols]
+            )
+
+        def round_res(u, cols):
+            dst, src = interleaved(res_bf[u][:, cols, :], res[u][:, :, cols])
+            nc.vector.tensor_copy(out=dst, in_=src)
+
+        def quantize_res(u, cols):
+            c, a = divmod(u, GROUPS)
+            nc.vector.quantize_mx(
+                out=res_codes[u][:, cols].bitcast(FP8X4),
+                scales=res_scales[c][:, a, cols],
+                in_=res_bf[u][:, cols, :].rearrange("p t j -> p (t j)"),
+            )
+
+        def store_codes(u):
+            c, a = divmod(u, GROUPS)
+            dst = out_1[a].rearrange("p t i -> p (t i)")[:, PACK * CHUNK * c : PACK * CHUNK * (c + 1)]
+            nc.sync.dma_start(out=dst.bitcast(I32), in_=res_codes[u][:])
+
+        def store_scales(c, queue):
+            for q in range(4):
+                dst = out_2[:, 4 * q : 4 * q + 4, CHUNK * c : CHUNK * (c + 1)].rearrange("a r t -> r a t")
+                queue.dma_start(
+                    out=dst.bitcast(I32), in_=res_scales[c][32 * q : 32 * q + 4, :, :].bitcast(I32)
+                )
+
+        whole = slice(0, CHUNK)
+
+        nc.vector.memset(scale_raw[:].bitcast(I32), 0)
+        load_scales(nc.scalar, w4_scales, 0)
+        load_x(0)
+        nc.sync.dma_start(out=w4_first[:].bitcast(I32), in_=w4_bytes[:, 0 : 2 * GROUP].bitcast(I32))
+        load_x(1)
+        nc.sync.dma_start(out=w8_first[:], in_=w8_bytes[:, 0 : 4 * GROUP].bitcast(I32))
+        load_scales(nc.sync, w8_scales, W8_ROW)
+        load_x(2)
+        nc.sync.dma_start(out=w4_rest[:].bitcast(I32), in_=w4_bytes[:, 2 * GROUP : 2 * M].bitcast(I32))
+        nc.sync.dma_start(out=w8_rest[:], in_=w8_bytes[:, 4 * GROUP : 4 * M].bitcast(I32))
+        load_x(3)
+
+        feature_on_vector(0, 0)
+        feature_on_scalar(1, 0)
+        deal_w4(0)
+        feature_on_vector(0, 1)
+        feature_on_scalar(1, 1)
+        deal_scales(0)
+        quantize_feature(0, 0)
+        deal_w8(0)
+        quantize_feature(1, 0)
+        feature_on_scalar(1, 2)
+        for r in range(PACK):
+            pass_w4(r)
+        for r in range(PACK):
+            pass_w8(r)
+        feature_on_vector(0, 2)
+        deal_w4(1)
+        deal_w8(1)
+        deal_scales(1)
+        for r in range(PACK):
+            both_passes(PACK + r)
+        deal_w4(2)
+        deal_w8(2)
+        deal_scales(2)
+        feature_on_vector(0, 3)
+        feature_on_vector(1, 3)
+        quantize_feature(0, 1)
+        quantize_feature(1, 1)
+
+        def one(r):
+            return slice(r, r + 1)
+
+        last = UNITS - 1
+        for u in range(last):
+            b = PACK * u
+            shared = u > 0
+            drain(b, False)
+            if shared:
+                square(u - 1, one(2 if u > 1 else 3), whole, False)
+                store_res(u - 1, slice(2, 4), whole)
+                round_res(u - 1, whole)
+            drain(b + 1, False)
+            square(u, one(0), whole, False)
+            drain(b + 2, False)
+            square(u, one(1), whole, False)
+            store_res(u, slice(0, 2), whole)
+            drain(b + 3, shared)
+            if shared:
+                quantize_res(u - 1, whole)
+                store_codes(u - 1)
+                if u == GROUPS:
+                    store_scales(0, nc.sync)
+                square(u, one(3), whole, True)
+            else:
+                square(u, one(2), whole, False)
+
+        b = PACK * last
+        drain(b, False)
+        square(last - 1, one(2), whole, False)
+        store_res(last - 1, slice(2, 4), whole)
+        round_res(last - 1, whole)
+        drain(b + 1, False)
+        drain(b + 2, False)
+        drain(b + 3, True)
+        quantize_res(last - 1, whole)
+        store_codes(last - 1)
+        square(last, one(3), whole, True)
+        halves = (slice(0, HALF), slice(HALF, CHUNK))
+        for cols in halves:
+            square(last, slice(0, 3), cols, False)
+            store_res(last, slice(0, 4), cols)
+        for cols in halves:
+            round_res(last, cols)
+        for cols in halves:
+            quantize_res(last, cols)
+        store_codes(last)
+        store_scales(CHUNKS - 1, nc.scalar)

@@ -37,7 +37,7 @@ def tile_mix_feat_fm_crelupl_relu2_kernel(
 
     with ExitStack() as ctx:
         keep = ctx.enter_context(tc.tile_pool(name="keep", bufs=1))
-        psum = ctx.enter_context(tc.psum_pool(name="psum", bufs=BANKS))
+        psum = ctx.enter_context(tc.psum_pool(name="psum", bufs=2))
         ctx.enter_context(tc.manual_schedule())
 
         def sbuf(name, shape, dtype):
@@ -47,8 +47,7 @@ def tile_mix_feat_fm_crelupl_relu2_kernel(
         feat = [[sbuf("feat%d_%d" % (s, c), [P, CHUNK, PACK], BF16) for c in range(CHUNKS)] for s in range(2)]
         feat_codes = [[sbuf("fcode%d_%d" % (s, c), [P, CHUNK], I32) for c in range(CHUNKS)] for s in range(2)]
         feat_scales = [[sbuf("fscale%d_%d" % (s, c), [P, CHUNK], U8) for c in range(CHUNKS)] for s in range(2)]
-        w4_first = sbuf("w4_first", [P, 2 * GROUP], U8)
-        w4_rest = sbuf("w4_rest", [P, 2 * (M - GROUP)], U8)
+        w4_raw = sbuf("w4_raw", [P, 2 * M], U8)
         w8_first = sbuf("w8_first", [P, GROUP], I32)
         w8_rest = sbuf("w8_rest", [P, M - GROUP], I32)
         scale_raw = sbuf("scale_raw", [P, M], U8)
@@ -59,7 +58,8 @@ def tile_mix_feat_fm_crelupl_relu2_kernel(
         res = [sbuf("res%d" % u, [P, PACK, CHUNK], F32) for u in range(UNITS)]
         res_bf = [sbuf("res_bf%d" % u, [P, CHUNK, PACK], BF16) for u in range(UNITS)]
         res_codes = [sbuf("res_codes%d" % u, [P, CHUNK], I32) for u in range(UNITS)]
-        res_scales = [sbuf("res_scales%d" % c, [P, GROUPS, CHUNK], U8) for c in range(CHUNKS)]
+        early_scales = sbuf("early_scales", [P, 1, T], U8)
+        last_scales = sbuf("last_scales", [P, GROUPS - 1, T], U8)
         acc = {}
 
         def load_x(h):
@@ -100,7 +100,7 @@ def tile_mix_feat_fm_crelupl_relu2_kernel(
             )
 
         def deal_w4(a):
-            src = w4_first[:] if a == 0 else w4_rest[:, 2 * GROUP * (a - 1) : 2 * GROUP * a]
+            src = w4_raw[:, 2 * GROUP * a : 2 * GROUP * (a + 1)]
             nc.vector.tensor_copy(
                 out=w4_dealt[a][:].rearrange("p (r m b) -> p r m b", r=PACK, b=2),
                 in_=src.rearrange("p (m r b) -> p r m b", r=PACK, b=2),
@@ -120,9 +120,9 @@ def tile_mix_feat_fm_crelupl_relu2_kernel(
             )
 
         def pass_w4(b):
-            c, a = divmod(b // PACK, GROUPS)
+            a, c = divmod(b // PACK, CHUNKS)
             r = b % PACK
-            acc[b] = psum.tile([P, CHUNK], F32, name="acc")
+            acc[b] = psum.tile([P, CHUNK], F32, name="acc%d" % r)
             nc.tensor.matmul_mx(
                 out=acc[b][:],
                 lhsT=w4_dealt[a][:, 2 * P * r : 2 * P * (r + 1)].bitcast(FP4X4),
@@ -134,7 +134,7 @@ def tile_mix_feat_fm_crelupl_relu2_kernel(
             )
 
         def pass_w8(b):
-            c, a = divmod(b // PACK, GROUPS)
+            a, c = divmod(b // PACK, CHUNKS)
             r = b % PACK
             nc.tensor.matmul_mx(
                 out=acc[b][:],
@@ -167,7 +167,7 @@ def tile_mix_feat_fm_crelupl_relu2_kernel(
                 nc.scalar.activation(out=res[u][:, rows, cols], in_=src, func=ACT.Square)
 
         def store_res(u, rows, cols):
-            c, a = divmod(u, GROUPS)
+            a, c = divmod(u, CHUNKS)
             dst = out_0[GROUP * a : GROUP * (a + 1), CHUNK * c : CHUNK * (c + 1)]
             nc.sync.dma_start(
                 out=dst.rearrange("(p r) t -> p r t", r=PACK)[:, rows, cols], in_=res[u][:, rows, cols]
@@ -178,112 +178,101 @@ def tile_mix_feat_fm_crelupl_relu2_kernel(
             nc.vector.tensor_copy(out=dst, in_=src)
 
         def quantize_res(u, cols):
-            c, a = divmod(u, GROUPS)
+            a, c = divmod(u, CHUNKS)
+            plane = early_scales[:, 0, :] if a == 0 else last_scales[:, a - 1, :]
             nc.vector.quantize_mx(
                 out=res_codes[u][:, cols].bitcast(FP8X4),
-                scales=res_scales[c][:, a, cols],
+                scales=plane[:, CHUNK * c + cols.start : CHUNK * c + cols.stop],
                 in_=res_bf[u][:, cols, :].rearrange("p t j -> p (t j)"),
             )
 
-        def store_codes(u):
-            c, a = divmod(u, GROUPS)
-            dst = out_1[a].rearrange("p t i -> p (t i)")[:, PACK * CHUNK * c : PACK * CHUNK * (c + 1)]
-            nc.sync.dma_start(out=dst.bitcast(I32), in_=res_codes[u][:])
+        def store_codes(u, cols):
+            a, c = divmod(u, CHUNKS)
+            dst = out_1[a].rearrange("p t i -> p (t i)").bitcast(I32)[:, CHUNK * c : CHUNK * (c + 1)]
+            nc.sync.dma_start(out=dst[:, cols], in_=res_codes[u][:, cols])
 
-        def store_scales(c, queue):
+        def store_scales(tile, groups, queues):
             for q in range(4):
-                dst = out_2[:, 4 * q : 4 * q + 4, CHUNK * c : CHUNK * (c + 1)].rearrange("a r t -> r a t")
-                queue.dma_start(
-                    out=dst.bitcast(I32), in_=res_scales[c][32 * q : 32 * q + 4, :, :].bitcast(I32)
-                )
+                dst = out_2[groups, 4 * q : 4 * q + 4, :].rearrange("a r t -> r a t")
+                queues[q].dma_start(out=dst.bitcast(I32), in_=tile[32 * q : 32 * q + 4, :, :].bitcast(I32))
+
+        def one(r):
+            return slice(r, r + 1)
 
         whole = slice(0, CHUNK)
 
         nc.vector.memset(scale_raw[:].bitcast(I32), 0)
         load_scales(nc.scalar, w4_scales, 0)
+        nc.sync.dma_start(out=w4_raw[:].bitcast(I32), in_=w4_bytes.bitcast(I32))
         load_x(0)
-        nc.sync.dma_start(out=w4_first[:].bitcast(I32), in_=w4_bytes[:, 0 : 2 * GROUP].bitcast(I32))
         load_x(1)
         nc.sync.dma_start(out=w8_first[:], in_=w8_bytes[:, 0 : 4 * GROUP].bitcast(I32))
         load_scales(nc.sync, w8_scales, W8_ROW)
         load_x(2)
-        nc.sync.dma_start(out=w4_rest[:].bitcast(I32), in_=w4_bytes[:, 2 * GROUP : 2 * M].bitcast(I32))
-        nc.sync.dma_start(out=w8_rest[:], in_=w8_bytes[:, 4 * GROUP : 4 * M].bitcast(I32))
         load_x(3)
+        nc.sync.dma_start(out=w8_rest[:], in_=w8_bytes[:, 4 * GROUP : 4 * M].bitcast(I32))
 
+        for h in range(2 * CHUNKS):
+            feature_on_scalar(1, h)
+        for a in range(GROUPS):
+            deal_w4(a)
         feature_on_vector(0, 0)
-        feature_on_scalar(1, 0)
-        deal_w4(0)
         feature_on_vector(0, 1)
-        feature_on_scalar(1, 1)
-        deal_scales(0)
-        quantize_feature(0, 0)
         deal_w8(0)
+        quantize_feature(0, 0)
+        deal_scales(0)
         quantize_feature(1, 0)
-        feature_on_scalar(1, 2)
         for r in range(PACK):
-            pass_w4(r)
-        for r in range(PACK):
-            pass_w8(r)
+            both_passes(r)
         feature_on_vector(0, 2)
-        deal_w4(1)
-        deal_w8(1)
-        deal_scales(1)
-        for r in range(PACK):
-            both_passes(PACK + r)
-        deal_w4(2)
-        deal_w8(2)
-        deal_scales(2)
         feature_on_vector(0, 3)
-        feature_on_vector(1, 3)
+        deal_scales(1)
         quantize_feature(0, 1)
         quantize_feature(1, 1)
+        for r in range(PACK):
+            both_passes(PACK + r)
+        deal_w8(1)
 
-        def one(r):
-            return slice(r, r + 1)
+        def square_and_store(u, r, on_vector):
+            square(u, one(r), whole, on_vector)
+            store_res(u, one(r), whole)
 
         last = UNITS - 1
-        for u in range(last):
+        drain(3, True)
+        deal_w8(2)
+        for u in range(UNITS):
             b = PACK * u
-            shared = u > 0
             drain(b, False)
-            if shared:
-                square(u - 1, one(2 if u > 1 else 3), whole, False)
-                store_res(u - 1, slice(2, 4), whole)
+            if u > 0:
                 round_res(u - 1, whole)
             drain(b + 1, False)
-            square(u, one(0), whole, False)
-            drain(b + 2, False)
-            square(u, one(1), whole, False)
-            store_res(u, slice(0, 2), whole)
-            drain(b + 3, shared)
-            if shared:
+            if u < last:
+                square_and_store(u, 0, False)
+            square_and_store(u, 3, True)
+            if u > 0:
                 quantize_res(u - 1, whole)
-                store_codes(u - 1)
-                if u == GROUPS:
-                    store_scales(0, nc.sync)
-                square(u, one(3), whole, True)
             else:
-                square(u, one(2), whole, False)
+                deal_scales(2)
+            drain(b + 2, False)
+            if u < last:
+                square_and_store(u, 1, False)
+            if u > 0:
+                store_codes(u - 1, whole)
+            if u == CHUNKS:
+                store_scales(early_scales, slice(0, 1), [nc.sync] * 4)
+            if u < last:
+                drain(b + PACK + 3, True)
+                square_and_store(u, 2, False)
 
-        b = PACK * last
-        drain(b, False)
-        square(last - 1, one(2), whole, False)
-        store_res(last - 1, slice(2, 4), whole)
-        round_res(last - 1, whole)
-        drain(b + 1, False)
-        drain(b + 2, False)
-        drain(b + 3, True)
-        quantize_res(last - 1, whole)
-        store_codes(last - 1)
-        square(last, one(3), whole, True)
-        halves = (slice(0, HALF), slice(HALF, CHUNK))
-        for cols in halves:
+        pieces = [slice(t, t + 128) for t in range(0, CHUNK, 128)]
+        for cols in pieces:
             square(last, slice(0, 3), cols, False)
-            store_res(last, slice(0, 4), cols)
-        for cols in halves:
+            if cols.stop % HALF == 0:
+                store_res(last, slice(0, 3), slice(cols.stop - HALF, cols.stop))
+        round_res(last, pieces[0])
+        for before, cols in zip(pieces, pieces[1:]):
             round_res(last, cols)
-        for cols in halves:
-            quantize_res(last, cols)
-        store_codes(last)
-        store_scales(CHUNKS - 1, nc.scalar)
+            quantize_res(last, before)
+        quantize_res(last, pieces[-1])
+        store_codes(last, whole)
+        store_scales(last_scales, slice(1, GROUPS), [nc.scalar, nc.scalar, nc.sync, nc.sync])

@@ -202,8 +202,8 @@ def tile_mix_feat_fm_crelupl_relu2_kernel(
         whole = slice(0, CHUNK)
 
         nc.vector.memset(scale_raw[:].bitcast(I32), 0)
-        load_scales(nc.scalar, w4_scales, 0)
         nc.sync.dma_start(out=w4_raw[:].bitcast(I32), in_=w4_bytes.bitcast(I32))
+        load_scales(nc.sync, w4_scales, 0)
         load_x(0)
         load_x(1)
         nc.sync.dma_start(out=w8_first[:], in_=w8_bytes[:, 0 : 4 * GROUP].bitcast(I32))

@@ -21,7 +21,8 @@ GROUPS = M // GROUP
 CHUNK = 512
 CHUNKS = T // CHUNK
 HALF = CHUNK // 2
-RUN = 4
+RUN = 2
+WORDS = 4
 UNITS = GROUPS * CHUNKS
 BANKS = 8
 W8_ROW = 4
@@ -109,8 +110,8 @@ def tile_mix_feat_fm_crelupl_relu2_kernel(
         def deal_w8(a):
             src = w8_first[:] if a == 0 else w8_rest[:, GROUP * (a - 1) : GROUP * a]
             nc.vector.tensor_copy(
-                out=w8_dealt[a][:].rearrange("p (r c e) -> p c r e", r=PACK, e=RUN),
-                in_=src.rearrange("p (c e r) -> p c r e", r=PACK, e=RUN),
+                out=w8_dealt[a][:].rearrange("p (r c e) -> p c r e", r=PACK, e=WORDS),
+                in_=src.rearrange("p (c e r) -> p c r e", r=PACK, e=WORDS),
             )
 
         def deal_scales(a):
@@ -214,9 +215,9 @@ def tile_mix_feat_fm_crelupl_relu2_kernel(
 
         for h in range(2 * CHUNKS):
             feature_on_scalar(1, h)
-        for a in range(GROUPS):
-            deal_w4(a)
+        deal_w4(0)
         feature_on_vector(0, 0)
+        deal_w4(1)
         feature_on_vector(0, 1)
         deal_w8(0)
         quantize_feature(0, 0)
@@ -238,8 +239,9 @@ def tile_mix_feat_fm_crelupl_relu2_kernel(
             store_res(u, one(r), whole)
 
         last = UNITS - 1
-        drain(3, True)
         deal_w8(2)
+        drain(3, True)
+        deal_w4(2)
         for u in range(UNITS):
             b = PACK * u
             drain(b, False)

@@ -21,11 +21,14 @@ GROUPS = M // GROUP
 CHUNK = 512
 CHUNKS = T // CHUNK
 HALF = CHUNK // 2
-RUN = 2
-WORDS = 4
 UNITS = GROUPS * CHUNKS
 BANKS = 8
+QUADRANTS = 4
 W8_ROW = 4
+RUN = 2
+WORDS = 4
+VECTOR_ROW = 3
+LAST_PIECE = 128
 
 
 def tile_mix_feat_fm_crelupl_relu2_kernel(
@@ -38,7 +41,7 @@ def tile_mix_feat_fm_crelupl_relu2_kernel(
 
     with ExitStack() as ctx:
         keep = ctx.enter_context(tc.tile_pool(name="keep", bufs=1))
-        psum = ctx.enter_context(tc.psum_pool(name="psum", bufs=2))
+        psum = ctx.enter_context(tc.psum_pool(name="psum", bufs=BANKS // PACK))
         ctx.enter_context(tc.manual_schedule())
 
         def sbuf(name, shape, dtype):
@@ -66,10 +69,10 @@ def tile_mix_feat_fm_crelupl_relu2_kernel(
         def load_x(h):
             nc.sync.dma_start(out=x_raw[h][:], in_=x_rows[:, :, h * HALF : (h + 1) * HALF])
 
-        def load_scales(queue, src, row):
-            for q in range(4):
-                queue.dma_start(
-                    out=scale_raw[32 * q + row : 32 * q + row + 4, :].bitcast(I32),
+        def load_scales(src, first_row):
+            for q in range(QUADRANTS):
+                nc.sync.dma_start(
+                    out=scale_raw[32 * q + first_row : 32 * q + first_row + 4, :].bitcast(I32),
                     in_=src[0, 4 * q : 4 * q + 4, :].bitcast(I32),
                 )
 
@@ -83,15 +86,13 @@ def tile_mix_feat_fm_crelupl_relu2_kernel(
             c, part = divmod(h, 2)
             return interleaved(feat[s][c][:, part * HALF : (part + 1) * HALF, :], x_raw[h][:])
 
-        def feature_on_vector(s, h):
-            dst, src = feature_views(s, h)
-            nc.vector.tensor_scalar(
-                out=dst, in0=src, scalar1=(1.0, -1.0)[s], scalar2=0.0, op0=ALU.mult, op1=ALU.max
-            )
+        def make_xa(h):
+            dst, src = feature_views(0, h)
+            nc.vector.tensor_scalar(out=dst, in0=src, scalar1=1.0, scalar2=0.0, op0=ALU.mult, op1=ALU.max)
 
-        def feature_on_scalar(s, h):
-            dst, src = feature_views(s, h)
-            nc.scalar.activation(out=dst, in_=src, func=ACT.Relu, scale=(1.0, -1.0)[s])
+        def make_xb(h):
+            dst, src = feature_views(1, h)
+            nc.scalar.activation(out=dst, in_=src, func=ACT.Relu, scale=-1.0)
 
         def quantize_feature(s, c):
             nc.vector.quantize_mx(
@@ -120,7 +121,7 @@ def tile_mix_feat_fm_crelupl_relu2_kernel(
                 in_=scale_raw[:, GROUP * a : GROUP * (a + 1)].rearrange("p (m r) -> p r m", r=PACK),
             )
 
-        def pass_w4(b):
+        def multiply(b):
             a, c = divmod(b // PACK, CHUNKS)
             r = b % PACK
             acc[b] = psum.tile([P, CHUNK], F32, name="acc%d" % r)
@@ -133,10 +134,6 @@ def tile_mix_feat_fm_crelupl_relu2_kernel(
                 start=True,
                 stop=False,
             )
-
-        def pass_w8(b):
-            a, c = divmod(b // PACK, CHUNKS)
-            r = b % PACK
             nc.tensor.matmul_mx(
                 out=acc[b][:],
                 lhsT=w8_dealt[a][:, P * r : P * (r + 1)].bitcast(FP8X4),
@@ -147,25 +144,21 @@ def tile_mix_feat_fm_crelupl_relu2_kernel(
                 stop=True,
             )
 
-        def both_passes(b):
-            if b < UNITS * PACK:
-                pass_w4(b)
-                pass_w8(b)
-
-        def drain(b, on_vector):
-            u, r = divmod(b, PACK)
-            if on_vector:
+        def drain(u, r):
+            b = PACK * u + r
+            if r == VECTOR_ROW:
                 nc.vector.tensor_scalar_max(out=relu[u][:, r, :], in0=acc[b][:], scalar1=0.0)
             else:
                 nc.scalar.activation(out=relu[u][:, r, :], in_=acc[b][:], func=ACT.Relu)
-            both_passes(b + BANKS)
+            if b + BANKS < UNITS * PACK:
+                multiply(b + BANKS)
 
-        def square(u, rows, cols, on_vector):
-            src = relu[u][:, rows, cols]
-            if on_vector:
-                nc.vector.tensor_tensor(out=res[u][:, rows, cols], in0=src, in1=src, op=ALU.mult)
-            else:
-                nc.scalar.activation(out=res[u][:, rows, cols], in_=src, func=ACT.Square)
+        def square_on_vector(u):
+            src = relu[u][:, one(VECTOR_ROW), :]
+            nc.vector.tensor_tensor(out=res[u][:, one(VECTOR_ROW), :], in0=src, in1=src, op=ALU.mult)
+
+        def square_on_scalar(u, rows, cols):
+            nc.scalar.activation(out=res[u][:, rows, cols], in_=relu[u][:, rows, cols], func=ACT.Square)
 
         def store_res(u, rows, cols):
             a, c = divmod(u, CHUNKS)
@@ -174,107 +167,108 @@ def tile_mix_feat_fm_crelupl_relu2_kernel(
                 out=dst.rearrange("(p r) t -> p r t", r=PACK)[:, rows, cols], in_=res[u][:, rows, cols]
             )
 
+        def square_and_store(u, r):
+            square_on_scalar(u, one(r), whole)
+            store_res(u, one(r), whole)
+
         def round_res(u, cols):
             dst, src = interleaved(res_bf[u][:, cols, :], res[u][:, :, cols])
             nc.vector.tensor_copy(out=dst, in_=src)
 
         def quantize_res(u, cols):
             a, c = divmod(u, CHUNKS)
-            plane = early_scales[:, 0, :] if a == 0 else last_scales[:, a - 1, :]
+            group_scales = early_scales[:, 0, :] if a == 0 else last_scales[:, a - 1, :]
             nc.vector.quantize_mx(
                 out=res_codes[u][:, cols].bitcast(FP8X4),
-                scales=plane[:, CHUNK * c + cols.start : CHUNK * c + cols.stop],
+                scales=group_scales[:, CHUNK * c + cols.start : CHUNK * c + cols.stop],
                 in_=res_bf[u][:, cols, :].rearrange("p t j -> p (t j)"),
             )
 
-        def store_codes(u, cols):
+        def store_codes(u):
             a, c = divmod(u, CHUNKS)
             dst = out_1[a].rearrange("p t i -> p (t i)").bitcast(I32)[:, CHUNK * c : CHUNK * (c + 1)]
-            nc.sync.dma_start(out=dst[:, cols], in_=res_codes[u][:, cols])
+            nc.sync.dma_start(out=dst, in_=res_codes[u][:])
 
-        def store_scales(tile, groups, queues):
-            for q in range(4):
+        def store_scales(src, groups):
+            for q in range(QUADRANTS):
                 dst = out_2[groups, 4 * q : 4 * q + 4, :].rearrange("a r t -> r a t")
-                queues[q].dma_start(out=dst.bitcast(I32), in_=tile[32 * q : 32 * q + 4, :, :].bitcast(I32))
+                nc.sync.dma_start(out=dst.bitcast(I32), in_=src[32 * q : 32 * q + 4, :, :].bitcast(I32))
 
         def one(r):
             return slice(r, r + 1)
 
         whole = slice(0, CHUNK)
+        last = UNITS - 1
 
         nc.vector.memset(scale_raw[:].bitcast(I32), 0)
         nc.sync.dma_start(out=w4_raw[:].bitcast(I32), in_=w4_bytes.bitcast(I32))
-        load_scales(nc.sync, w4_scales, 0)
+        load_scales(w4_scales, 0)
         load_x(0)
         load_x(1)
         nc.sync.dma_start(out=w8_first[:], in_=w8_bytes[:, 0 : 4 * GROUP].bitcast(I32))
-        load_scales(nc.sync, w8_scales, W8_ROW)
+        load_scales(w8_scales, W8_ROW)
         load_x(2)
         load_x(3)
         nc.sync.dma_start(out=w8_rest[:], in_=w8_bytes[:, 4 * GROUP : 4 * M].bitcast(I32))
 
         for h in range(2 * CHUNKS):
-            feature_on_scalar(1, h)
+            make_xb(h)
         deal_w4(0)
-        feature_on_vector(0, 0)
+        make_xa(0)
         deal_w4(1)
-        feature_on_vector(0, 1)
+        make_xa(1)
         deal_w8(0)
         quantize_feature(0, 0)
         deal_scales(0)
         quantize_feature(1, 0)
         for r in range(PACK):
-            both_passes(r)
-        feature_on_vector(0, 2)
-        feature_on_vector(0, 3)
+            multiply(r)
+        make_xa(2)
+        make_xa(3)
         deal_scales(1)
         quantize_feature(0, 1)
         quantize_feature(1, 1)
         for r in range(PACK):
-            both_passes(PACK + r)
+            multiply(PACK + r)
         deal_w8(1)
-
-        def square_and_store(u, r, on_vector):
-            square(u, one(r), whole, on_vector)
-            store_res(u, one(r), whole)
-
-        last = UNITS - 1
         deal_w8(2)
-        drain(3, True)
+        drain(0, VECTOR_ROW)
         deal_w4(2)
+
         for u in range(UNITS):
-            b = PACK * u
-            drain(b, False)
+            drain(u, 0)
             if u > 0:
                 round_res(u - 1, whole)
-            drain(b + 1, False)
+            drain(u, 1)
             if u < last:
-                square_and_store(u, 0, False)
-            square_and_store(u, 3, True)
+                square_and_store(u, 0)
+            square_on_vector(u)
             if u > 0:
                 quantize_res(u - 1, whole)
             else:
                 deal_scales(2)
-            drain(b + 2, False)
+            drain(u, 2)
             if u < last:
-                square_and_store(u, 1, False)
+                square_and_store(u, 1)
+            store_res(u, one(VECTOR_ROW), whole)
             if u > 0:
-                store_codes(u - 1, whole)
+                store_codes(u - 1)
             if u == CHUNKS:
-                store_scales(early_scales, slice(0, 1), [nc.sync] * 4)
+                store_scales(early_scales, slice(0, 1))
             if u < last:
-                drain(b + PACK + 3, True)
-                square_and_store(u, 2, False)
+                drain(u + 1, VECTOR_ROW)
+                square_and_store(u, 2)
 
-        pieces = [slice(t, t + 128) for t in range(0, CHUNK, 128)]
+        scalar_rows = slice(0, VECTOR_ROW)
+        pieces = [slice(t, t + LAST_PIECE) for t in range(0, CHUNK, LAST_PIECE)]
         for cols in pieces:
-            square(last, slice(0, 3), cols, False)
+            square_on_scalar(last, scalar_rows, cols)
             if cols.stop % HALF == 0:
-                store_res(last, slice(0, 3), slice(cols.stop - HALF, cols.stop))
+                store_res(last, scalar_rows, slice(cols.stop - HALF, cols.stop))
         round_res(last, pieces[0])
         for before, cols in zip(pieces, pieces[1:]):
             round_res(last, cols)
             quantize_res(last, before)
         quantize_res(last, pieces[-1])
-        store_codes(last, whole)
-        store_scales(last_scales, slice(1, GROUPS), [nc.scalar, nc.scalar, nc.sync, nc.sync])
+        store_codes(last)
+        store_scales(last_scales, slice(1, GROUPS))

from contextlib import ExitStack

import concourse.mybir as mybir

K, M, T = 512, 1536, 1024
FLOPS = 2 * 2 * K * M * T

F32 = mybir.dt.float32
BF16 = mybir.dt.bfloat16
I32 = mybir.dt.int32
U8 = mybir.dt.uint8
FP8X4 = mybir.dt.float8_e4m3fn_x4
FP4X4 = mybir.dt.float4_e2m1fn_x4
ALU = mybir.AluOpType
ACT = mybir.ActivationFunctionType

P = 128
PACK = 4
GROUP = P * PACK
GROUPS = M // GROUP
CHUNK = 512
CHUNKS = T // CHUNK
HALF = CHUNK // 2
UNITS = GROUPS * CHUNKS
BANKS = 8
QUADRANTS = 4
W8_ROW = 4
RUN = 2
WORDS = 4
VECTOR_ROW = 3
LAST_PIECE = 128


def tile_mix_feat_fm_crelupl_relu2_kernel(
    tc, x, w4_words, w4_scales, w8_words, w8_scales, out_0, out_1, out_2
):
    nc = tc.nc
    x_rows = x.rearrange("(p j) t -> p j t", j=PACK)
    w4_bytes = w4_words[0]
    w8_bytes = w8_words[0].rearrange("p n i -> p (n i)")

    with ExitStack() as ctx:
        keep = ctx.enter_context(tc.tile_pool(name="keep", bufs=1))
        psum = ctx.enter_context(tc.psum_pool(name="psum", bufs=BANKS // PACK))
        ctx.enter_context(tc.manual_schedule())

        def sbuf(name, shape, dtype):
            return keep.tile(shape, dtype, name=name, align_bytes=64)

        x_raw = [sbuf("x_raw%d" % h, [P, PACK, HALF], F32) for h in range(2 * CHUNKS)]
        feat = [[sbuf("feat%d_%d" % (s, c), [P, CHUNK, PACK], BF16) for c in range(CHUNKS)] for s in range(2)]
        feat_codes = [[sbuf("fcode%d_%d" % (s, c), [P, CHUNK], I32) for c in range(CHUNKS)] for s in range(2)]
        feat_scales = [[sbuf("fscale%d_%d" % (s, c), [P, CHUNK], U8) for c in range(CHUNKS)] for s in range(2)]
        w4_raw = sbuf("w4_raw", [P, 2 * M], U8)
        w8_first = sbuf("w8_first", [P, GROUP], I32)
        w8_rest = sbuf("w8_rest", [P, M - GROUP], I32)
        scale_raw = sbuf("scale_raw", [P, M], U8)
        w4_dealt = [sbuf("w4_dealt%d" % a, [P, 2 * GROUP], U8) for a in range(GROUPS)]
        w8_dealt = [sbuf("w8_dealt%d" % a, [P, GROUP], I32) for a in range(GROUPS)]
        scale_dealt = [sbuf("scale_dealt%d" % a, [P, GROUP], U8) for a in range(GROUPS)]
        relu = [sbuf("relu%d" % u, [P, PACK, CHUNK], F32) for u in range(UNITS)]
        res = [sbuf("res%d" % u, [P, PACK, CHUNK], F32) for u in range(UNITS)]
        res_bf = [sbuf("res_bf%d" % u, [P, CHUNK, PACK], BF16) for u in range(UNITS)]
        res_codes = [sbuf("res_codes%d" % u, [P, CHUNK], I32) for u in range(UNITS)]
        early_scales = sbuf("early_scales", [P, 1, T], U8)
        last_scales = sbuf("last_scales", [P, GROUPS - 1, T], U8)
        acc = {}

        def load_x(h):
            nc.sync.dma_start(out=x_raw[h][:], in_=x_rows[:, :, h * HALF : (h + 1) * HALF])

        def load_scales(src, first_row):
            for q in range(QUADRANTS):
                nc.sync.dma_start(
                    out=scale_raw[32 * q + first_row : 32 * q + first_row + 4, :].bitcast(I32),
                    in_=src[0, 4 * q : 4 * q + 4, :].bitcast(I32),
                )

        def interleaved(dst, src):
            return (
                dst.rearrange("p (c e) j -> p c j e", e=RUN),
                src.rearrange("p j (c e) -> p c j e", e=RUN),
            )

        def feature_views(s, h):
            c, part = divmod(h, 2)
            return interleaved(feat[s][c][:, part * HALF : (part + 1) * HALF, :], x_raw[h][:])

        def make_xa(h):
            dst, src = feature_views(0, h)
            nc.vector.tensor_scalar(out=dst, in0=src, scalar1=1.0, scalar2=0.0, op0=ALU.mult, op1=ALU.max)

        def make_xb(h):
            dst, src = feature_views(1, h)
            nc.scalar.activation(out=dst, in_=src, func=ACT.Relu, scale=-1.0)

        def quantize_feature(s, c):
            nc.vector.quantize_mx(
                out=feat_codes[s][c][:].bitcast(FP8X4),
                scales=feat_scales[s][c][:],
                in_=feat[s][c][:].rearrange("p t j -> p (t j)"),
            )

        def deal_w4(a):
            src = w4_raw[:, 2 * GROUP * a : 2 * GROUP * (a + 1)]
            nc.vector.tensor_copy(
                out=w4_dealt[a][:].rearrange("p (r m b) -> p r m b", r=PACK, b=2),
                in_=src.rearrange("p (m r b) -> p r m b", r=PACK, b=2),
            )

        def deal_w8(a):
            src = w8_first[:] if a == 0 else w8_rest[:, GROUP * (a - 1) : GROUP * a]
            nc.vector.tensor_copy(
                out=w8_dealt[a][:].rearrange("p (r c e) -> p c r e", r=PACK, e=WORDS),
                in_=src.rearrange("p (c e r) -> p c r e", r=PACK, e=WORDS),
            )

        def deal_scales(a):
            nc.vector.tensor_copy(
                out=scale_dealt[a][:].rearrange("p (r m) -> p r m", r=PACK),
                in_=scale_raw[:, GROUP * a : GROUP * (a + 1)].rearrange("p (m r) -> p r m", r=PACK),
            )

        def multiply(b):
            a, c = divmod(b // PACK, CHUNKS)
            r = b % PACK
            acc[b] = psum.tile([P, CHUNK], F32, name="acc%d" % r)
            nc.tensor.matmul_mx(
                out=acc[b][:],
                lhsT=w4_dealt[a][:, 2 * P * r : 2 * P * (r + 1)].bitcast(FP4X4),
                lhsT_scale=scale_dealt[a][:, P * r : P * (r + 1)],
                rhs=feat_codes[0][c][:].bitcast(FP8X4),
                rhs_scale=feat_scales[0][c][:],
                start=True,
                stop=False,
            )
            nc.tensor.matmul_mx(
                out=acc[b][:],
                lhsT=w8_dealt[a][:, P * r : P * (r + 1)].bitcast(FP8X4),
                lhsT_scale=scale_dealt[a][W8_ROW:P, P * r : P * (r + 1)],
                rhs=feat_codes[1][c][:].bitcast(FP8X4),
                rhs_scale=feat_scales[1][c][:],
                start=False,
                stop=True,
            )

        def drain(u, r):
            b = PACK * u + r
            if r == VECTOR_ROW:
                nc.vector.tensor_scalar_max(out=relu[u][:, r, :], in0=acc[b][:], scalar1=0.0)
            else:
                nc.scalar.activation(out=relu[u][:, r, :], in_=acc[b][:], func=ACT.Relu)
            if b + BANKS < UNITS * PACK:
                multiply(b + BANKS)

        def square_on_vector(u):
            src = relu[u][:, one(VECTOR_ROW), :]
            nc.vector.tensor_tensor(out=res[u][:, one(VECTOR_ROW), :], in0=src, in1=src, op=ALU.mult)

        def square_on_scalar(u, rows, cols):
            nc.scalar.activation(out=res[u][:, rows, cols], in_=relu[u][:, rows, cols], func=ACT.Square)

        def store_res(u, rows, cols):
            a, c = divmod(u, CHUNKS)
            dst = out_0[GROUP * a : GROUP * (a + 1), CHUNK * c : CHUNK * (c + 1)]
            nc.sync.dma_start(
                out=dst.rearrange("(p r) t -> p r t", r=PACK)[:, rows, cols], in_=res[u][:, rows, cols]
            )

        def square_and_store(u, r):
            square_on_scalar(u, one(r), whole)
            store_res(u, one(r), whole)

        def round_res(u, cols):
            dst, src = interleaved(res_bf[u][:, cols, :], res[u][:, :, cols])
            nc.vector.tensor_copy(out=dst, in_=src)

        def quantize_res(u, cols):
            a, c = divmod(u, CHUNKS)
            group_scales = early_scales[:, 0, :] if a == 0 else last_scales[:, a - 1, :]
            nc.vector.quantize_mx(
                out=res_codes[u][:, cols].bitcast(FP8X4),
                scales=group_scales[:, CHUNK * c + cols.start : CHUNK * c + cols.stop],
                in_=res_bf[u][:, cols, :].rearrange("p t j -> p (t j)"),
            )

        def store_codes(u):
            a, c = divmod(u, CHUNKS)
            dst = out_1[a].rearrange("p t i -> p (t i)").bitcast(I32)[:, CHUNK * c : CHUNK * (c + 1)]
            nc.sync.dma_start(out=dst, in_=res_codes[u][:])

        def store_scales(src, groups):
            for q in range(QUADRANTS):
                dst = out_2[groups, 4 * q : 4 * q + 4, :].rearrange("a r t -> r a t")
                nc.sync.dma_start(out=dst.bitcast(I32), in_=src[32 * q : 32 * q + 4, :, :].bitcast(I32))

        def one(r):
            return slice(r, r + 1)

        whole = slice(0, CHUNK)
        last = UNITS - 1

        nc.vector.memset(scale_raw[:].bitcast(I32), 0)
        nc.sync.dma_start(out=w4_raw[:].bitcast(I32), in_=w4_bytes.bitcast(I32))
        load_scales(w4_scales, 0)
        load_x(0)
        load_x(1)
        nc.sync.dma_start(out=w8_first[:], in_=w8_bytes[:, 0 : 4 * GROUP].bitcast(I32))
        load_scales(w8_scales, W8_ROW)
        load_x(2)
        load_x(3)
        nc.sync.dma_start(out=w8_rest[:], in_=w8_bytes[:, 4 * GROUP : 4 * M].bitcast(I32))

        for h in range(2 * CHUNKS):
            make_xb(h)
        deal_w4(0)
        make_xa(0)
        deal_w4(1)
        make_xa(1)
        deal_w8(0)
        quantize_feature(0, 0)
        deal_scales(0)
        quantize_feature(1, 0)
        for r in range(PACK):
            multiply(r)
        make_xa(2)
        make_xa(3)
        deal_scales(1)
        quantize_feature(0, 1)
        quantize_feature(1, 1)
        for r in range(PACK):
            multiply(PACK + r)
        deal_w8(1)
        deal_w8(2)
        drain(0, VECTOR_ROW)
        deal_w4(2)

        for u in range(UNITS):
            drain(u, 0)
            if u > 0:
                round_res(u - 1, whole)
            drain(u, 1)
            if u < last:
                square_and_store(u, 0)
            square_on_vector(u)
            if u > 0:
                quantize_res(u - 1, whole)
            else:
                deal_scales(2)
            drain(u, 2)
            if u < last:
                square_and_store(u, 1)
            store_res(u, one(VECTOR_ROW), whole)
            if u > 0:
                store_codes(u - 1)
            if u == CHUNKS:
                store_scales(early_scales, slice(0, 1))
            if u < last:
                drain(u + 1, VECTOR_ROW)
                square_and_store(u, 2)

        scalar_rows = slice(0, VECTOR_ROW)
        pieces = [slice(t, t + LAST_PIECE) for t in range(0, CHUNK, LAST_PIECE)]
        for cols in pieces:
            square_on_scalar(last, scalar_rows, cols)
            if cols.stop % HALF == 0:
                store_res(last, scalar_rows, slice(cols.stop - HALF, cols.stop))
        round_res(last, pieces[0])
        for before, cols in zip(pieces, pieces[1:]):
            round_res(last, cols)
            quantize_res(last, before)
        quantize_res(last, pieces[-1])
        store_codes(last)
        store_scales(last_scales, slice(1, GROUPS))
